import numpy as np
import ml_dtypes


def mxq(x, axis, fmt="e4m3"):
    dtype, down = {"e4m3": (ml_dtypes.float8_e4m3fn, 7), "e5m2": (ml_dtypes.float8_e5m2, 14)}[fmt]
    v = np.moveaxis(np.asarray(x, np.float32).astype(ml_dtypes.bfloat16).astype(np.float64), axis, -1)
    blocks = v.reshape(v.shape[:-1] + (-1, 32))
    amax = np.abs(blocks).max(-1, keepdims=True)
    byte = np.maximum(np.where(amax > 0, np.frexp(amax)[1] - 1 + 127, 0) - down, 1)
    scale = np.exp2(byte - 127.0)
    codes = (blocks / scale).astype(np.float32).astype(dtype).astype(np.float64)
    return np.moveaxis((codes * scale).reshape(v.shape), -1, axis)


WIDE = False


def mx_kscale(k):
    if not WIDE:
        return np.ones(k)
    levels = np.array([10, -10, 5, -5, 0])
    if k % 512:
        return np.exp2(np.random.permutation(np.resize(levels, k // 32))).repeat(32)
    a = np.empty((k // 512, 16))
    for p in range(k // 512):
        a[p, :8] = np.random.permutation(np.resize(levels, 8))
        for g in range(8):
            far = levels[np.abs(levels - a[p, g]) >= 10]
            a[p, g + 8] = far[np.random.randint(len(far))]
    return np.exp2(a.ravel()).repeat(32)


def f64(x):
    return np.asarray(x).astype(np.float64)


def striped(idx):
    return np.tile(idx.reshape(-1, 16).T, (8, 1)).astype(np.uint16)


def unstriped(offs):
    return offs[:16].T.reshape(-1).astype(np.int64)


def striped8(idx):
    return np.concatenate([x.reshape(-1, 16).T for x in idx]).astype(np.uint16)


def runs(offs, k):
    lists = np.stack([offs[16 * r : 16 * r + 16].T.reshape(-1) for r in range(8)]).astype(np.int64)
    return lists[np.arange(k) % 512 // 64]


def pack_weight(w):
    k, n = w.shape
    w = f64(np.asarray(w, np.float32).astype(ml_dtypes.bfloat16)).reshape(k // 32, 32, n)
    amax = np.abs(w).max(1)
    byte = np.clip(np.where(amax > 0, np.frexp(amax)[1] - 1 + 127 - 7, 1), 1, 254)
    scaled = (w * np.exp2(127.0 - byte)[:, None, :]).reshape(k, n).astype(np.float32)
    words = np.ascontiguousarray(scaled.reshape(k // 512, 128, 4, n).transpose(0, 1, 3, 2)).astype(ml_dtypes.float8_e4m3fn).view(np.uint8)
    return words, np.ascontiguousarray(byte.astype(np.uint8).reshape(k // 512, 16, n))


def unpack_weight(words, scales):
    g, p, n, _ = words.shape
    vals = np.ascontiguousarray(words).view(ml_dtypes.float8_e4m3fn).astype(np.float64) * np.repeat(np.exp2(scales.astype(np.float64) - 127.0), 8, axis=1)[..., None]
    return vals.transpose(0, 1, 3, 2).reshape(g * 512, n)


E2M1 = np.array([0.0, 0.5, 1.0, 1.5, 2.0, 3.0, 4.0, 6.0, -0.0, -0.5, -1.0, -1.5, -2.0, -3.0, -4.0, -6.0])


def pack_fp4(w):
    k, n = w.shape
    w = f64(np.asarray(w, np.float32).astype(ml_dtypes.bfloat16)).reshape(k // 32, 32, n)
    amax = np.abs(w).max(1)
    mant, ex = np.frexp(amax / 6.0)
    byte = np.clip(np.where(amax > 0, np.where(mant > 0.5, ex, ex - 1) + 127, 1), 1, 254)
    scaled = (w * np.exp2(127.0 - byte)[:, None, :]).reshape(k, n).astype(np.float32)
    c = np.ascontiguousarray(scaled.reshape(k // 512, 128, 4, n).transpose(0, 1, 3, 2)).astype(ml_dtypes.float4_e2m1fn).view(np.uint8) & 0xF
    words = (c[..., 0::2] | (c[..., 1::2] << 4)).reshape(k // 512, 128, 2 * n)
    return np.ascontiguousarray(words), np.ascontiguousarray(byte.astype(np.uint8).reshape(k // 512, 16, n))


def unpack_fp4(words, scales):
    g, _, n = scales.shape
    words = np.ascontiguousarray(words).reshape(g, 128, n, 2)
    nib = np.empty((g, 128, n, 4), np.uint8)
    nib[..., 0::2] = words & 0xF
    nib[..., 1::2] = words >> 4
    vals = E2M1[nib] * np.repeat(np.exp2(scales.astype(np.float64) - 127.0), 8, axis=1)[..., None]
    return vals.transpose(0, 1, 3, 2).reshape(g * 512, n)


def planes(y):
    n, m = y.shape
    v = y.astype(np.float32).astype(ml_dtypes.bfloat16).astype(np.float64).reshape(n // 32, 32, m)
    top = np.abs(v).max(1)
    byte = np.clip(np.where(top > 0, np.frexp(top)[1] - 1 + 127 - 7, 1), 1, 254)
    codes = (v * np.exp2(127.0 - byte)[:, None, :]).reshape(n, m).astype(np.float32).astype(ml_dtypes.float8_e4m3fn).view(np.uint8)
    words = codes.reshape(n // 512, 128, 4, m).transpose(0, 1, 3, 2)
    return np.ascontiguousarray(words), np.ascontiguousarray(byte.astype(np.uint8).reshape(n // 512, 16, m))


K, T, S, N, H = 512, 2048, 512, 512, 512


def setup_inputs():
    n = np.random.standard_normal
    s = mx_kscale(K)[:, None]
    u = mx_kscale(H)
    packed_xT = pack_weight(n((K, T)) * s)
    packed_w2 = pack_fp4(n((H, N)) / np.sqrt(H) / u[:, None])
    return {
        "x_words": packed_xT[0],
        "x_scales": packed_xT[1],
        "w1": (n((K, H)) / np.sqrt(K) / s * u).astype(np.float32),
        "up": np.clip(n((H, S)), 0.25, 1.0).astype(np.float32),
        "w2_words": packed_w2[0],
        "w2_scales": packed_w2[1],
        "offs": striped(np.random.permutation(T)[:S]),
        "mate": striped8(np.stack([np.random.permutation(S) for _ in range(8)])),
    }


def reference(x_words, x_scales, w1, up, w2_words, w2_scales, offs, mate):
    xq = unpack_weight(x_words, x_scales)[:, unstriped(offs)]
    y = mxq(f64(w1), 0, "e4m3").T @ xq
    o = y[np.arange(H)[:, None], runs(mate, H)]
    lo = np.minimum(y, o)
    z = lo + f64(up) * (np.maximum(y, o) - lo)
    out_0 = unpack_fp4(w2_words, w2_scales).T @ mxq(z, 0, "e4m3")
    return (out_0,) + planes(out_0)

@@ -1,0 +1,233 @@
+from contextlib import ExitStack
+
+import concourse.mybir as mybir
+
+K, T, S, H, N = 512, 2048, 512, 512, 512
+FLOPS = 2 * K * H * S + 2 * H * N * S
+
+F32 = mybir.dt.float32
+BF16 = mybir.dt.bfloat16
+I32 = mybir.dt.int32
+U32 = mybir.dt.uint32
+U16 = mybir.dt.uint16
+U8 = mybir.dt.uint8
+FP8X4 = mybir.dt.float8_e4m3fn_x4
+FP4X4 = mybir.dt.float4_e2m1fn_x4
+ALU = mybir.AluOpType
+ACT = mybir.ActivationFunctionType
+
+P = 128
+PACK = 4
+HALF = S // 2
+PIECE = 128
+
+
+def tile_picked_cmpex_none_po_kernel(
+    tc, x_words, x_scales, w1, up, w2_words, w2_scales, offs, mate, out_0, out_1, out_2
+):
+    nc = tc.nc
+    with ExitStack() as ctx:
+        keep = ctx.enter_context(tc.tile_pool(name="keep", bufs=1))
+        psum = ctx.enter_context(tc.psum_pool(name="psum", bufs=1))
+
+        offs_sb = keep.tile([P, S // 16], U16, name="offs_sb")
+        mate_sb = keep.tile([P, S // 16], U16, name="mate_sb")
+        xw_all = keep.tile([P, T], I32, name="xw_all", align_bytes=64)
+        xs_rows = keep.tile([P, T], U8, name="xs_rows", align_bytes=64)
+        xs_all = keep.tile([P, T], U8, name="xs_all", align_bytes=64)
+        w2w_raw = keep.tile([P, 2 * N], U8, name="w2w_raw", align_bytes=64)
+        w2s_raw = keep.tile([P, N], U8, name="w2s_raw", align_bytes=64)
+        w1_raw = [keep.tile([P, PACK, H // 2], F32, name="w1_raw%d" % h, align_bytes=64) for h in range(2)]
+        up_sb = [keep.tile([P, PACK, HALF], F32, name="up_sb%d" % h, align_bytes=64) for h in range(2)]
+
+        nc.vector.memset(xs_all[:].bitcast(I32), 0)
+        nc.vector.memset(w2s_raw[:].bitcast(I32), 0)
+
+        w1_rows = w1.rearrange("(p j) h -> p j h", j=PACK)
+        up_rows = up.rearrange("(p t) s -> p t s", t=PACK)
+        nc.sync.dma_start(offs_sb[:], offs)
+        for q in range(4):
+            nc.scalar.dma_start(out=xs_rows[32 * q : 32 * q + 4, :].bitcast(I32), in_=x_scales[0, 4 * q : 4 * q + 4, :].bitcast(I32))
+        nc.sync.dma_start(out=w2w_raw[:].bitcast(I32), in_=w2_words[0].bitcast(I32))
+        for h in range(2):
+            nc.sync.dma_start(out=w1_raw[h][:], in_=w1_rows[:, :, h * (H // 2) : (h + 1) * (H // 2)])
+        for q in range(4):
+            nc.sync.dma_start(out=w2s_raw[32 * q : 32 * q + 4, :].bitcast(I32), in_=w2_scales[0, 4 * q : 4 * q + 4, :].bitcast(I32))
+        nc.sync.dma_start(out=xw_all[:], in_=x_words[0].rearrange("p c r -> p (c r)").bitcast(I32))
+        nc.sync.dma_start(mate_sb[:], mate)
+        for h in range(2):
+            nc.sync.dma_start(out=up_sb[h][:], in_=up_rows[:, :, h * HALF : (h + 1) * HALF])
+
+        for q in range(4):
+            nc.vector.tensor_copy(out=xs_all[32 * q : 32 * q + 4, :].bitcast(I32), in_=xs_rows[32 * q : 32 * q + 4, :].bitcast(I32))
+
+        w2w = keep.tile([P, 2 * N], U8, name="w2w", align_bytes=64)
+        w2s = keep.tile([P, N], U8, name="w2s", align_bytes=64)
+        nc.vector.tensor_copy(
+            out=w2w[:].rearrange("p (t m b) -> p m t b", t=PACK, b=2),
+            in_=w2w_raw[:].rearrange("p (m t b) -> p m t b", t=PACK, b=2),
+        )
+
+        w1_bf = keep.tile([P, PACK, P, PACK], BF16, name="w1_bf", align_bytes=64)
+        views = [
+            (
+                w1_bf[:, :, h * 64 : (h + 1) * 64, :].rearrange("p t m j -> p m j t"),
+                w1_raw[h][:].rearrange("p j (m t) -> p m j t", t=PACK),
+            )
+            for h in range(2)
+        ]
+        nc.scalar.activation(out=views[0][0], in_=views[0][1], func=ACT.Copy)
+
+        xs = keep.tile([P, S], U8, name="xs", align_bytes=64)
+        nc.vector.tensor_copy(xs[:], xs_all[:].indirect(offs_sb[:]))
+        nc.scalar.activation(out=views[1][0], in_=views[1][1], func=ACT.Copy)
+        w1c = keep.tile([P, H], U32, name="w1c", align_bytes=64)
+        w1s = keep.tile([P, H], U8, name="w1s", align_bytes=64)
+        nc.vector.quantize_mx(out=w1c[:].bitcast(FP8X4), scales=w1s[:], in_=w1_bf[:].rearrange("p t m j -> p (t m j)"))
+
+        nc.vector.tensor_copy(
+            out=w2s[:].rearrange("p (t m) -> p m t", t=PACK),
+            in_=w2s_raw[:].rearrange("p (m t) -> p m t", t=PACK),
+        )
+        xw = [keep.tile([P, HALF], U32, name="xw%d" % h, align_bytes=64) for h in range(2)]
+        y_win = [keep.tile([P, S], F32, name="y_win%d" % t, align_bytes=64) for t in range(PACK)]
+        y_own = [keep.tile([P, PACK, HALF], F32, name="y_own%d" % h, align_bytes=64) for h in range(2)]
+        diff = [keep.tile([P, PACK, HALF], F32, name="diff%d" % h, align_bytes=64) for h in range(2)]
+        mag = [keep.tile([P, PACK, HALF], F32, name="mag%d" % h, align_bytes=64) for h in range(2)]
+        mid = [keep.tile([P, PACK, HALF], F32, name="mid%d" % h, align_bytes=64) for h in range(2)]
+        lift = [keep.tile([P, PACK, HALF], F32, name="lift%d" % h, align_bytes=64) for h in range(2)]
+        zb = keep.tile([P, S, PACK], BF16, name="zb", align_bytes=64)
+        zc = keep.tile([P, S], U32, name="zc", align_bytes=64)
+        zs = keep.tile([P, S], U8, name="zs", align_bytes=64)
+        res = keep.tile([P, PACK, S], F32, name="res", align_bytes=64)
+        rb = keep.tile([P, S, PACK], BF16, name="rb", align_bytes=64)
+        oc = keep.tile([P, S], U32, name="oc", align_bytes=64)
+        osc = keep.tile([P, S], U8, name="osc", align_bytes=64)
+        out_rows = out_0.rearrange("(p t) s -> p t s", t=PACK)
+        out_words = out_1[0].rearrange("p c r -> p (c r)").bitcast(I32)
+
+        def first_product(t, h):
+            bank = psum.tile([P, HALF], F32, name="y_bank", tag="bank%d" % (2 * t + h))
+            nc.tensor.matmul_mx(
+                out=bank[:],
+                lhsT=w1c[:, t * P : (t + 1) * P].bitcast(FP8X4),
+                lhsT_scale=w1s[:, t * P : (t + 1) * P],
+                rhs=xw[h][:].bitcast(FP8X4),
+                rhs_scale=xs[:, h * HALF : (h + 1) * HALF],
+                start=True,
+                stop=True,
+            )
+            nc.scalar.copy(out=y_win[t][:, h * HALF : (h + 1) * HALF], in_=bank[:])
+            if h == 0:
+                nc.scalar.copy(out=y_own[0][:, t, :], in_=bank[:])
+            else:
+                nc.sync.dma_start(out=y_own[1][:, t, :], in_=y_win[t][:, HALF:S])
+
+        def fetch(h, t):
+            nc.vector.tensor_tensor(
+                diff[h][:, t, :], y_win[t][:].indirect(mate_sb[:, h * 16 : (h + 1) * 16]), y_own[h][:, t, :], ALU.subtract
+            )
+
+        def magnitude(h, ts, js):
+            nc.scalar.activation(out=mag[h][:, ts, js], in_=diff[h][:, ts, js], func=ACT.Abs)
+
+        def middle(h, ts, js):
+            nc.vector.scalar_tensor_tensor(
+                out=mid[h][:, ts, js], in0=diff[h][:, ts, js], scalar=0.5, in1=y_own[h][:, ts, js], op0=ALU.mult, op1=ALU.add
+            )
+
+        def share(h, ts, js):
+            nc.vector.scalar_tensor_tensor(
+                out=lift[h][:, ts, js], in0=up_sb[h][:, ts, js], scalar=0.5, in1=mag[h][:, ts, js], op0=ALU.subtract, op1=ALU.mult
+            )
+
+        def mix(c):
+            h, js = c // 2, slice((c % 2) * PIECE, (c % 2 + 1) * PIECE)
+            nc.vector.tensor_tensor(
+                zb[:, c * PIECE : (c + 1) * PIECE, :].rearrange("p (a i) t -> p a t i", i=4),
+                mid[h][:, :, js].rearrange("p t (a i) -> p a t i", i=4),
+                lift[h][:, :, js].rearrange("p t (a i) -> p a t i", i=4),
+                ALU.add,
+            )
+
+        def quantise(codes, scales, values, cols):
+            nc.vector.quantize_mx(out=codes[:, cols].bitcast(FP8X4), scales=scales[:, cols], in_=values[:, cols, :].rearrange("p s t -> p (s t)"))
+
+        def pass_two(dst, t, cols):
+            nc.tensor.matmul_mx(
+                out=dst,
+                lhsT=w2w[:, 2 * t * P : 2 * (t + 1) * P].bitcast(FP4X4),
+                lhsT_scale=w2s[:, t * P : (t + 1) * P],
+                rhs=zc[:, cols].bitcast(FP8X4),
+                rhs_scale=zs[:, cols],
+                start=True,
+                stop=True,
+            )
+
+        def second_product(c):
+            cols = slice(c * PIECE, (c + 1) * PIECE)
+            quantise(zc, zs, zb, cols)
+            if c < 3:
+                bank = psum.tile([P, PACK, PIECE], F32, name="o_bank", tag="bank%d" % (2 * c))
+                for t in range(PACK):
+                    pass_two(bank[:, t, :], t, cols)
+                nc.scalar.copy(out=res[:, :, cols], in_=bank[:])
+                nc.scalar.copy(out=rb[:, cols, :], in_=bank[:].rearrange("p t s -> p s t"))
+            else:
+                for pair in range(2):
+                    bank = psum.tile([P, 2, PIECE], F32, name="o_bank", tag="bank%d" % (6 + pair))
+                    for u in range(2):
+                        pass_two(bank[:, u, :], 2 * pair + u, cols)
+                    nc.scalar.copy(out=res[:, 2 * pair : 2 * pair + 2, cols], in_=bank[:])
+                nc.vector.tensor_copy(
+                    out=rb[:, cols, :].rearrange("p (a i) t -> p a t i", i=4),
+                    in_=res[:, :, cols].rearrange("p t (a i) -> p a t i", i=4),
+                )
+
+        def store_values(cols):
+            nc.sync.dma_start(out=out_rows[:, :, cols], in_=res[:, :, cols])
+
+        def store_words(cols):
+            quantise(oc, osc, rb, cols)
+            nc.sync.dma_start(out=out_words[:, cols], in_=oc[:, cols].bitcast(I32))
+
+        every = slice(0, HALF)
+        all_t = slice(0, PACK)
+        for h in range(2):
+            nc.vector.tensor_copy(xw[h][:], xw_all[:].bitcast(U32).indirect(offs_sb[:, h * 16 : (h + 1) * 16]))
+        for t in range(PACK):
+            first_product(t, 0)
+            first_product(t, 1)
+            fetch(0, t)
+            middle(0, slice(t, t + 1), every)
+        magnitude(0, slice(0, 2), every)
+        magnitude(0, slice(2, 4), every)
+        share(0, slice(0, 2), every)
+        fetch(1, 0)
+        share(0, slice(2, 4), every)
+        fetch(1, 1)
+        magnitude(1, slice(0, 2), every)
+        mix(0)
+        fetch(1, 2)
+        second_product(0)
+        mix(1)
+        fetch(1, 3)
+        magnitude(1, slice(2, 4), every)
+        second_product(1)
+        store_values(slice(0, 256))
+        middle(1, all_t, slice(0, 128))
+        share(1, all_t, slice(0, 128))
+        middle(1, all_t, slice(128, 256))
+        mix(2)
+        share(1, all_t, slice(128, 256))
+        second_product(2)
+        store_values(slice(256, 384))
+        mix(3)
+        store_words(slice(0, 256))
+        second_product(3)
+        store_values(slice(384, 512))
+        store_words(slice(256, 384))
+        store_words(slice(384, 512))
+        for q in range(4):
+            queue = nc.sync if q % 2 == 0 else nc.scalar
+            queue.dma_start(out=out_2[0, 4 * q : 4 * q + 4, :].bitcast(I32), in_=osc[32 * q : 32 * q + 4, :].bitcast(I32))

@@ -28,68 +28,59 @@ def tile_picked_cmpex_none_po_kernel(
     nc = tc.nc
     with ExitStack() as ctx:
         keep = ctx.enter_context(tc.tile_pool(name="keep", bufs=1))
+        shared = ctx.enter_context(tc.tile_pool(name="shared", bufs=1))
         psum = ctx.enter_context(tc.psum_pool(name="psum", bufs=1))
 
         offs_sb = keep.tile([P, S // 16], U16, name="offs_sb")
         mate_sb = keep.tile([P, S // 16], U16, name="mate_sb")
-        xw_all = keep.tile([P, T], I32, name="xw_all", align_bytes=64)
+        xw_all = shared.tile([P, T], I32, name="xw_all", offset=0, align_bytes=64)
         xs_rows = keep.tile([P, T], U8, name="xs_rows", align_bytes=64)
         xs_all = keep.tile([P, T], U8, name="xs_all", align_bytes=64)
         w2w_raw = keep.tile([P, 2 * N], U8, name="w2w_raw", align_bytes=64)
         w2s_raw = keep.tile([P, N], U8, name="w2s_raw", align_bytes=64)
-        w1_raw = [keep.tile([P, PACK, H // 2], F32, name="w1_raw%d" % h, align_bytes=64) for h in range(2)]
-        up_sb = [keep.tile([P, PACK, HALF], F32, name="up_sb%d" % h, align_bytes=64) for h in range(2)]
+        w1_raw = keep.tile([P, PACK, H], F32, name="w1_raw", tag="wide", align_bytes=64)
 
-        nc.vector.memset(xs_all[:].bitcast(I32), 0)
         nc.vector.memset(w2s_raw[:].bitcast(I32), 0)
+        nc.vector.memset(xs_all[:].bitcast(I32), 0)
 
         w1_rows = w1.rearrange("(p j) h -> p j h", j=PACK)
         up_rows = up.rearrange("(p t) s -> p t s", t=PACK)
+        for q in range(4):
+            queue = nc.sync if q % 2 == 0 else nc.scalar
+            queue.dma_start(out=xs_rows[32 * q : 32 * q + 4, :].bitcast(I32), in_=x_scales[0, 4 * q : 4 * q + 4, :].bitcast(I32))
         nc.sync.dma_start(offs_sb[:], offs)
-        for q in range(4):
-            nc.scalar.dma_start(out=xs_rows[32 * q : 32 * q + 4, :].bitcast(I32), in_=x_scales[0, 4 * q : 4 * q + 4, :].bitcast(I32))
-        nc.sync.dma_start(out=w2w_raw[:].bitcast(I32), in_=w2_words[0].bitcast(I32))
-        for h in range(2):
-            nc.sync.dma_start(out=w1_raw[h][:], in_=w1_rows[:, :, h * (H // 2) : (h + 1) * (H // 2)])
-        for q in range(4):
-            nc.sync.dma_start(out=w2s_raw[32 * q : 32 * q + 4, :].bitcast(I32), in_=w2_scales[0, 4 * q : 4 * q + 4, :].bitcast(I32))
+        nc.sync.dma_start(out=w1_raw[:], in_=w1_rows)
         nc.sync.dma_start(out=xw_all[:], in_=x_words[0].rearrange("p c r -> p (c r)").bitcast(I32))
         nc.sync.dma_start(mate_sb[:], mate)
-        for h in range(2):
-            nc.sync.dma_start(out=up_sb[h][:], in_=up_rows[:, :, h * HALF : (h + 1) * HALF])
+        nc.sync.dma_start(out=w2w_raw[:].bitcast(I32), in_=w2_words[0].bitcast(I32))
+        for q in range(4):
+            nc.sync.dma_start(out=w2s_raw[32 * q : 32 * q + 4, :].bitcast(I32), in_=w2_scales[0, 4 * q : 4 * q + 4, :].bitcast(I32))
 
         for q in range(4):
-            nc.vector.tensor_copy(out=xs_all[32 * q : 32 * q + 4, :].bitcast(I32), in_=xs_rows[32 * q : 32 * q + 4, :].bitcast(I32))
+            mover = nc.vector if q % 2 == 0 else nc.gpsimd
+            mover.tensor_copy(out=xs_all[32 * q : 32 * q + 4, :].bitcast(I32), in_=xs_rows[32 * q : 32 * q + 4, :].bitcast(I32))
 
-        w2w = keep.tile([P, 2 * N], U8, name="w2w", align_bytes=64)
-        w2s = keep.tile([P, N], U8, name="w2s", align_bytes=64)
-        nc.vector.tensor_copy(
-            out=w2w[:].rearrange("p (t m b) -> p m t b", t=PACK, b=2),
-            in_=w2w_raw[:].rearrange("p (m t b) -> p m t b", t=PACK, b=2),
-        )
-
-        w1_bf = keep.tile([P, PACK, P, PACK], BF16, name="w1_bf", align_bytes=64)
+        w1_bf = keep.tile([P, PACK, P, PACK], BF16, name="w1_bf", tag="first", align_bytes=64)
         views = [
             (
-                w1_bf[:, :, h * 64 : (h + 1) * 64, :].rearrange("p t m j -> p m j t"),
-                w1_raw[h][:].rearrange("p j (m t) -> p m j t", t=PACK),
+                w1_bf[:, :, ms, :].rearrange("p t m j -> p m j t"),
+                w1_raw[:].rearrange("p j (m t) -> p m j t", t=PACK)[:, ms, :, :],
             )
-            for h in range(2)
+            for ms in (slice(0, 80), slice(80, P))
         ]
         nc.scalar.activation(out=views[0][0], in_=views[0][1], func=ACT.Copy)
 
         xs = keep.tile([P, S], U8, name="xs", align_bytes=64)
         nc.vector.tensor_copy(xs[:], xs_all[:].indirect(offs_sb[:]))
-        nc.scalar.activation(out=views[1][0], in_=views[1][1], func=ACT.Copy)
+        nc.vector.tensor_copy(out=views[1][0], in_=views[1][1])
+        up_sb = keep.tile([P, PACK, S], F32, name="up_sb", tag="wide", align_bytes=64)
+        for u in range(2):
+            nc.sync.dma_start(out=up_sb[:, 2 * u : 2 * u + 2, :], in_=up_rows[:, 2 * u : 2 * u + 2, :])
         w1c = keep.tile([P, H], U32, name="w1c", align_bytes=64)
         w1s = keep.tile([P, H], U8, name="w1s", align_bytes=64)
         nc.vector.quantize_mx(out=w1c[:].bitcast(FP8X4), scales=w1s[:], in_=w1_bf[:].rearrange("p t m j -> p (t m j)"))
 
-        nc.vector.tensor_copy(
-            out=w2s[:].rearrange("p (t m) -> p m t", t=PACK),
-            in_=w2s_raw[:].rearrange("p (m t) -> p m t", t=PACK),
-        )
-        xw = [keep.tile([P, HALF], U32, name="xw%d" % h, align_bytes=64) for h in range(2)]
+        xw = [keep.tile([P, HALF], U32, name="xw%d" % h, tag=tag, align_bytes=64) for h, tag in enumerate(("first", "second"))]
         y_win = [keep.tile([P, S], F32, name="y_win%d" % t, align_bytes=64) for t in range(PACK)]
         y_own = [keep.tile([P, PACK, HALF], F32, name="y_own%d" % h, align_bytes=64) for h in range(2)]
         diff = [keep.tile([P, PACK, HALF], F32, name="diff%d" % h, align_bytes=64) for h in range(2)]
@@ -138,15 +129,15 @@ def tile_picked_cmpex_none_po_kernel(
 
         def share(h, ts, js):
             nc.vector.scalar_tensor_tensor(
-                out=lift[h][:, ts, js], in0=up_sb[h][:, ts, js], scalar=0.5, in1=mag[h][:, ts, js], op0=ALU.subtract, op1=ALU.mult
+                out=lift[h][:, ts, js], in0=up_sb[:, ts, h * HALF + js.start : h * HALF + js.stop], scalar=0.5, in1=mag[h][:, ts, js], op0=ALU.subtract, op1=ALU.mult
             )
 
         def mix(c):
             h, js = c // 2, slice((c % 2) * PIECE, (c % 2 + 1) * PIECE)
             nc.vector.tensor_tensor(
-                zb[:, c * PIECE : (c + 1) * PIECE, :].rearrange("p (a i) t -> p a t i", i=4),
-                mid[h][:, :, js].rearrange("p t (a i) -> p a t i", i=4),
-                lift[h][:, :, js].rearrange("p t (a i) -> p a t i", i=4),
+                zb[:, c * PIECE : (c + 1) * PIECE, :].rearrange("p (a i) t -> p a t i", i=2),
+                mid[h][:, :, js].rearrange("p t (a i) -> p a t i", i=2),
+                lift[h][:, :, js].rearrange("p t (a i) -> p a t i", i=2),
                 ALU.add,
             )
 
@@ -180,8 +171,8 @@ def tile_picked_cmpex_none_po_kernel(
                         pass_two(bank[:, u, :], 2 * pair + u, cols)
                     nc.scalar.copy(out=res[:, 2 * pair : 2 * pair + 2, cols], in_=bank[:])
                 nc.vector.tensor_copy(
-                    out=rb[:, cols, :].rearrange("p (a i) t -> p a t i", i=4),
-                    in_=res[:, :, cols].rearrange("p t (a i) -> p a t i", i=4),
+                    out=rb[:, cols, :].rearrange("p (a i) t -> p a t i", i=2),
+                    in_=res[:, :, cols].rearrange("p t (a i) -> p a t i", i=2),
                 )
 
         def store_values(cols):
@@ -195,6 +186,17 @@ def tile_picked_cmpex_none_po_kernel(
         all_t = slice(0, PACK)
         for h in range(2):
             nc.vector.tensor_copy(xw[h][:], xw_all[:].bitcast(U32).indirect(offs_sb[:, h * 16 : (h + 1) * 16]))
+        w2w = shared.tile([P, 2 * N], U8, name="w2w", offset=0, align_bytes=64)
+        nc.vector.tensor_copy(
+            out=w2w[:].rearrange("p (t m b) -> p t m b", t=PACK, b=2),
+            in_=w2w_raw[:].rearrange("p (m t b) -> p t m b", t=PACK, b=2),
+        )
+
+        w2s = shared.tile([P, N], U8, name="w2s", offset=2 * N, align_bytes=64)
+        nc.vector.tensor_copy(
+            out=w2s[:].rearrange("p (t m) -> p t m", t=PACK),
+            in_=w2s_raw[:].rearrange("p (m t) -> p t m", t=PACK),
+        )
         for t in range(PACK):
             first_product(t, 0)
             first_product(t, 1)

@@ -60,13 +60,13 @@ def tile_picked_cmpex_none_po_kernel(
             mover = nc.vector if q % 2 == 0 else nc.gpsimd
             mover.tensor_copy(out=xs_all[32 * q : 32 * q + 4, :].bitcast(I32), in_=xs_rows[32 * q : 32 * q + 4, :].bitcast(I32))
 
-        w1_bf = keep.tile([P, PACK, P, PACK], BF16, name="w1_bf", tag="first", align_bytes=64)
+        w1_bf = shared.tile([P, PACK, P, PACK], BF16, name="w1_bf", offset=4 * T, align_bytes=64)
         views = [
             (
                 w1_bf[:, :, ms, :].rearrange("p t m j -> p m j t"),
                 w1_raw[:].rearrange("p j (m t) -> p m j t", t=PACK)[:, ms, :, :],
             )
-            for ms in (slice(0, 80), slice(80, P))
+            for ms in (slice(0, 48), slice(48, P))
         ]
         nc.scalar.activation(out=views[0][0], in_=views[0][1], func=ACT.Copy)
 
@@ -80,7 +80,7 @@ def tile_picked_cmpex_none_po_kernel(
         w1s = keep.tile([P, H], U8, name="w1s", align_bytes=64)
         nc.vector.quantize_mx(out=w1c[:].bitcast(FP8X4), scales=w1s[:], in_=w1_bf[:].rearrange("p t m j -> p (t m j)"))
 
-        xw = [keep.tile([P, HALF], U32, name="xw%d" % h, tag=tag, align_bytes=64) for h, tag in enumerate(("first", "second"))]
+        xw = [shared.tile([P, HALF], U32, name="xw%d" % h, offset=4 * T + 4 * HALF * h, align_bytes=64) for h in range(2)]
         y_win = [keep.tile([P, S], F32, name="y_win%d" % t, align_bytes=64) for t in range(PACK)]
         y_own = [keep.tile([P, PACK, HALF], F32, name="y_own%d" % h, align_bytes=64) for h in range(2)]
         diff = [keep.tile([P, PACK, HALF], F32, name="diff%d" % h, align_bytes=64) for h in range(2)]
@@ -109,10 +109,13 @@ def tile_picked_cmpex_none_po_kernel(
                 stop=True,
             )
             nc.scalar.copy(out=y_win[t][:, h * HALF : (h + 1) * HALF], in_=bank[:])
-            if h == 0:
-                nc.scalar.copy(out=y_own[0][:, t, :], in_=bank[:])
-            else:
-                nc.sync.dma_start(out=y_own[1][:, t, :], in_=y_win[t][:, HALF:S])
+            return bank
+
+        def own_first(t, bank):
+            nc.scalar.copy(out=y_own[0][:, t, :], in_=bank[:])
+
+        def own_second(t):
+            nc.sync.dma_start(out=y_own[1][:, t, :], in_=y_win[t][:, HALF:S])
 
         def fetch(h, t):
             nc.vector.tensor_tensor(
@@ -158,22 +161,27 @@ def tile_picked_cmpex_none_po_kernel(
         def second_product(c):
             cols = slice(c * PIECE, (c + 1) * PIECE)
             quantise(zc, zs, zb, cols)
-            if c < 3:
+            if c < 2:
                 bank = psum.tile([P, PACK, PIECE], F32, name="o_bank", tag="bank%d" % (2 * c))
                 for t in range(PACK):
                     pass_two(bank[:, t, :], t, cols)
                 nc.scalar.copy(out=res[:, :, cols], in_=bank[:])
-                nc.scalar.copy(out=rb[:, cols, :], in_=bank[:].rearrange("p t s -> p s t"))
+                nc.scalar.copy(
+                    out=rb[:, cols, :].rearrange("p (a i) t -> p a t i", i=2),
+                    in_=bank[:].rearrange("p t (a i) -> p a t i", i=2),
+                )
             else:
                 for pair in range(2):
-                    bank = psum.tile([P, 2, PIECE], F32, name="o_bank", tag="bank%d" % (6 + pair))
+                    bank = psum.tile([P, 2, PIECE], F32, name="o_bank", tag="bank%d" % (2 * c + pair))
                     for u in range(2):
                         pass_two(bank[:, u, :], 2 * pair + u, cols)
                     nc.scalar.copy(out=res[:, 2 * pair : 2 * pair + 2, cols], in_=bank[:])
-                nc.vector.tensor_copy(
-                    out=rb[:, cols, :].rearrange("p (a i) t -> p a t i", i=2),
-                    in_=res[:, :, cols].rearrange("p t (a i) -> p a t i", i=2),
-                )
+
+        def round_values(cols):
+            nc.vector.tensor_copy(
+                out=rb[:, cols, :].rearrange("p (a i) t -> p a t i", i=2),
+                in_=res[:, :, cols].rearrange("p t (a i) -> p a t i", i=2),
+            )
 
         def store_values(cols):
             nc.sync.dma_start(out=out_rows[:, :, cols], in_=res[:, :, cols])
@@ -197,27 +205,35 @@ def tile_picked_cmpex_none_po_kernel(
             out=w2s[:].rearrange("p (t m) -> p t m", t=PACK),
             in_=w2s_raw[:].rearrange("p (m t) -> p t m", t=PACK),
         )
+        own_first(0, first_product(0, 0))
+        ahead = first_product(1, 0)
         for t in range(PACK):
-            first_product(t, 0)
+            if t > 1:
+                own_first(t, first_product(t, 0))
             first_product(t, 1)
+            if t == 0:
+                own_first(1, ahead)
+            own_second(t)
             fetch(0, t)
-            middle(0, slice(t, t + 1), every)
+            if t > 0:
+                middle(0, slice(t - 1, t), every)
         magnitude(0, slice(0, 2), every)
         magnitude(0, slice(2, 4), every)
+        middle(0, slice(3, 4), every)
         share(0, slice(0, 2), every)
         fetch(1, 0)
         share(0, slice(2, 4), every)
         fetch(1, 1)
         magnitude(1, slice(0, 2), every)
-        mix(0)
         fetch(1, 2)
-        second_product(0)
-        mix(1)
+        mix(0)
         fetch(1, 3)
         magnitude(1, slice(2, 4), every)
+        second_product(0)
+        mix(1)
+        middle(1, all_t, slice(0, 128))
         second_product(1)
         store_values(slice(0, 256))
-        middle(1, all_t, slice(0, 128))
         share(1, all_t, slice(0, 128))
         middle(1, all_t, slice(128, 256))
         mix(2)
@@ -228,8 +244,9 @@ def tile_picked_cmpex_none_po_kernel(
         store_words(slice(0, 256))
         second_product(3)
         store_values(slice(384, 512))
-        store_words(slice(256, 384))
-        store_words(slice(384, 512))
+        for cols in (slice(256, 384), slice(384, 512)):
+            round_values(cols)
+            store_words(cols)
         for q in range(4):
             queue = nc.sync if q % 2 == 0 else nc.scalar
             queue.dma_start(out=out_2[0, 4 * q : 4 * q + 4, :].bitcast(I32), in_=osc[32 * q : 32 * q + 4, :].bitcast(I32))

@@ -1,6 +1,7 @@
 from contextlib import ExitStack
 
 import concourse.mybir as mybir
+from concourse.masks import make_identity
 
 K, T, S, H, N = 512, 2048, 512, 512, 512
 FLOPS = 2 * K * H * S + 2 * H * N * S
@@ -57,8 +58,7 @@ def tile_picked_cmpex_none_po_kernel(
             nc.sync.dma_start(out=w2s_raw[32 * q : 32 * q + 4, :].bitcast(I32), in_=w2_scales[0, 4 * q : 4 * q + 4, :].bitcast(I32))
 
         for q in range(4):
-            mover = nc.vector if q % 2 == 0 else nc.gpsimd
-            mover.tensor_copy(out=xs_all[32 * q : 32 * q + 4, :].bitcast(I32), in_=xs_rows[32 * q : 32 * q + 4, :].bitcast(I32))
+            nc.vector.tensor_copy(out=xs_all[32 * q : 32 * q + 4, :].bitcast(I32), in_=xs_rows[32 * q : 32 * q + 4, :].bitcast(I32))
 
         w1_bf = shared.tile([P, PACK, P, PACK], BF16, name="w1_bf", offset=4 * T, align_bytes=64)
         views = [
@@ -87,7 +87,10 @@ def tile_picked_cmpex_none_po_kernel(
         mag = [keep.tile([P, PACK, HALF], F32, name="mag%d" % h, align_bytes=64) for h in range(2)]
         mid = [keep.tile([P, PACK, HALF], F32, name="mid%d" % h, align_bytes=64) for h in range(2)]
         lift = [keep.tile([P, PACK, HALF], F32, name="lift%d" % h, align_bytes=64) for h in range(2)]
-        zb = keep.tile([P, S, PACK], BF16, name="zb", align_bytes=64)
+        zb = [keep.tile([P, PIECE, PACK], BF16, name="zb%d" % c, align_bytes=64) for c in range(4)]
+        zt = [keep.tile([P, 2, P, 2], BF16, name="zt%d" % c, align_bytes=64) for c in range(2)]
+        ident = keep.tile([P, P], F32, name="ident", align_bytes=64)
+        make_identity(nc, ident[:])
         zc = keep.tile([P, S], U32, name="zc", align_bytes=64)
         zs = keep.tile([P, S], U8, name="zs", align_bytes=64)
         res = keep.tile([P, PACK, S], F32, name="res", align_bytes=64)
@@ -138,14 +141,33 @@ def tile_picked_cmpex_none_po_kernel(
         def mix(c):
             h, js = c // 2, slice((c % 2) * PIECE, (c % 2 + 1) * PIECE)
             nc.vector.tensor_tensor(
-                zb[:, c * PIECE : (c + 1) * PIECE, :].rearrange("p (a i) t -> p a t i", i=2),
+                zb[c][:].rearrange("p (a i) t -> p a t i", i=2),
                 mid[h][:, :, js].rearrange("p t (a i) -> p a t i", i=2),
                 lift[h][:, :, js].rearrange("p t (a i) -> p a t i", i=2),
                 ALU.add,
             )
 
+        def add_turned(bank, c, t):
+            js = slice(c * PIECE, (c + 1) * PIECE)
+            nc.tensor.matmul(bank[:, t, :], mid[0][:, t, js], ident[:], start=True, stop=False, is_transpose=True)
+            nc.tensor.matmul(bank[:, t, :], lift[0][:, t, js], ident[:], start=False, stop=True, is_transpose=True)
+
+        def turn_back(bank, c):
+            nc.scalar.copy(
+                out=zt[c][:].rearrange("j u (a i) e -> j u a e i", i=4),
+                in_=bank[:].rearrange("j (u e) (a i) -> j u a e i", e=2, i=4),
+            )
+            words = zt[c][:].rearrange("j u p e -> j u (p e)").bitcast(F32)
+            back = psum.tile([P, 2, PIECE], F32, name="back", tag="bank%d" % (2 * c))
+            for u in range(2):
+                nc.tensor.transpose(back[:, u, :], words[:, u, :], ident[:])
+            nc.scalar.copy(
+                out=zb[c][:].rearrange("p s t -> p (s t)").bitcast(F32).rearrange("p (a i u) -> p a u i", i=2, u=2),
+                in_=back[:].rearrange("p u (a i) -> p a u i", i=2),
+            )
+
         def quantise(codes, scales, values, cols):
-            nc.vector.quantize_mx(out=codes[:, cols].bitcast(FP8X4), scales=scales[:, cols], in_=values[:, cols, :].rearrange("p s t -> p (s t)"))
+            nc.vector.quantize_mx(out=codes[:, cols].bitcast(FP8X4), scales=scales[:, cols], in_=values.rearrange("p s t -> p (s t)"))
 
         def pass_two(dst, t, cols):
             nc.tensor.matmul_mx(
@@ -160,16 +182,17 @@ def tile_picked_cmpex_none_po_kernel(
 
         def second_product(c):
             cols = slice(c * PIECE, (c + 1) * PIECE)
-            quantise(zc, zs, zb, cols)
+            quantise(zc, zs, zb[c][:], cols)
             if c < 2:
                 bank = psum.tile([P, PACK, PIECE], F32, name="o_bank", tag="bank%d" % (2 * c))
                 for t in range(PACK):
                     pass_two(bank[:, t, :], t, cols)
                 nc.scalar.copy(out=res[:, :, cols], in_=bank[:])
-                nc.scalar.copy(
-                    out=rb[:, cols, :].rearrange("p (a i) t -> p a t i", i=2),
-                    in_=bank[:].rearrange("p t (a i) -> p a t i", i=2),
-                )
+                if c == 0:
+                    nc.scalar.copy(
+                        out=rb[:, cols, :].rearrange("p (a i) t -> p a t i", i=2),
+                        in_=bank[:].rearrange("p t (a i) -> p a t i", i=2),
+                    )
             else:
                 for pair in range(2):
                     bank = psum.tile([P, 2, PIECE], F32, name="o_bank", tag="bank%d" % (2 * c + pair))
@@ -187,7 +210,7 @@ def tile_picked_cmpex_none_po_kernel(
             nc.sync.dma_start(out=out_rows[:, :, cols], in_=res[:, :, cols])
 
         def store_words(cols):
-            quantise(oc, osc, rb, cols)
+            quantise(oc, osc, rb[:, cols, :], cols)
             nc.sync.dma_start(out=out_words[:, cols], in_=oc[:, cols].bitcast(I32))
 
         every = slice(0, HALF)
@@ -220,31 +243,35 @@ def tile_picked_cmpex_none_po_kernel(
         magnitude(0, slice(0, 2), every)
         magnitude(0, slice(2, 4), every)
         middle(0, slice(3, 4), every)
-        share(0, slice(0, 2), every)
-        fetch(1, 0)
-        share(0, slice(2, 4), every)
-        fetch(1, 1)
+        turned = [psum.tile([P, PACK, P], F32, name="turned", tag="bank%d" % (2 * c + 1)) for c in range(2)]
+        for pair in range(2):
+            share(0, slice(2 * pair, 2 * pair + 2), every)
+            for c in range(2):
+                for t in (2 * pair, 2 * pair + 1):
+                    add_turned(turned[c], c, t)
+            fetch(1, pair)
         magnitude(1, slice(0, 2), every)
         fetch(1, 2)
-        mix(0)
+        turn_back(turned[0], 0)
         fetch(1, 3)
         magnitude(1, slice(2, 4), every)
-        second_product(0)
-        mix(1)
+        turn_back(turned[1], 1)
         middle(1, all_t, slice(0, 128))
-        second_product(1)
-        store_values(slice(0, 256))
-        share(1, all_t, slice(0, 128))
         middle(1, all_t, slice(128, 256))
-        mix(2)
+        share(1, all_t, slice(0, 128))
+        second_product(0)
+        store_values(slice(0, 128))
         share(1, all_t, slice(128, 256))
+        mix(2)
+        second_product(1)
+        store_values(slice(128, 256))
+        mix(3)
         second_product(2)
         store_values(slice(256, 384))
-        mix(3)
-        store_words(slice(0, 256))
         second_product(3)
         store_values(slice(384, 512))
-        for cols in (slice(256, 384), slice(384, 512)):
+        store_words(slice(0, 128))
+        for cols in (slice(128, 384), slice(384, 512)):
             round_values(cols)
             store_words(cols)
         for q in range(4):

@@ -19,8 +19,12 @@ ACT = mybir.ActivationFunctionType
 
 P = 128
 PACK = 4
+QUADRANTS = 4
+ALIGN = 64
+LIST_ROWS = 16
 HALF = S // 2
 PIECE = 128
+SCALAR_GROUPS = 48
 
 
 def tile_picked_cmpex_none_po_kernel(
@@ -32,76 +36,93 @@ def tile_picked_cmpex_none_po_kernel(
         shared = ctx.enter_context(tc.tile_pool(name="shared", bufs=1))
         psum = ctx.enter_context(tc.psum_pool(name="psum", bufs=1))
 
-        offs_sb = keep.tile([P, S // 16], U16, name="offs_sb")
-        mate_sb = keep.tile([P, S // 16], U16, name="mate_sb")
-        xw_all = shared.tile([P, T], I32, name="xw_all", offset=0, align_bytes=64)
-        xs_rows = keep.tile([P, T], U8, name="xs_rows", align_bytes=64)
-        xs_all = keep.tile([P, T], U8, name="xs_all", align_bytes=64)
-        w2w_raw = keep.tile([P, 2 * N], U8, name="w2w_raw", align_bytes=64)
-        w2s_raw = keep.tile([P, N], U8, name="w2s_raw", align_bytes=64)
-        w1_raw = keep.tile([P, PACK, H], F32, name="w1_raw", tag="wide", align_bytes=64)
+        def scale_rows(tile, q):
+            return tile[32 * q : 32 * q + 4, :].bitcast(I32)
+
+        def small_queue(q):
+            return nc.sync if q % 2 == 0 else nc.scalar
+
+        offs_sb = keep.tile([P, S // LIST_ROWS], U16, name="offs_sb")
+        mate_sb = keep.tile([P, S // LIST_ROWS], U16, name="mate_sb")
+        xw_all = shared.tile([P, T], I32, name="xw_all", offset=0, align_bytes=ALIGN)
+        xs_rows = keep.tile([P, T], U8, name="xs_rows", align_bytes=ALIGN)
+        xs_all = keep.tile([P, T], U8, name="xs_all", align_bytes=ALIGN)
+        w2w_raw = keep.tile([P, 2 * N], U8, name="w2w_raw", align_bytes=ALIGN)
+        w2s_raw = keep.tile([P, N], U8, name="w2s_raw", align_bytes=ALIGN)
+        w1_raw = keep.tile([P, PACK, H], F32, name="w1_raw", tag="wide", align_bytes=ALIGN)
 
         nc.vector.memset(w2s_raw[:].bitcast(I32), 0)
         nc.vector.memset(xs_all[:].bitcast(I32), 0)
 
         w1_rows = w1.rearrange("(p j) h -> p j h", j=PACK)
         up_rows = up.rearrange("(p t) s -> p t s", t=PACK)
-        for q in range(4):
-            queue = nc.sync if q % 2 == 0 else nc.scalar
-            queue.dma_start(out=xs_rows[32 * q : 32 * q + 4, :].bitcast(I32), in_=x_scales[0, 4 * q : 4 * q + 4, :].bitcast(I32))
+        for q in range(QUADRANTS):
+            small_queue(q).dma_start(out=scale_rows(xs_rows, q), in_=x_scales[0, 4 * q : 4 * q + 4, :].bitcast(I32))
         nc.sync.dma_start(offs_sb[:], offs)
         nc.sync.dma_start(out=w1_raw[:], in_=w1_rows)
         nc.sync.dma_start(out=xw_all[:], in_=x_words[0].rearrange("p c r -> p (c r)").bitcast(I32))
         nc.sync.dma_start(mate_sb[:], mate)
         nc.sync.dma_start(out=w2w_raw[:].bitcast(I32), in_=w2_words[0].bitcast(I32))
-        for q in range(4):
-            nc.sync.dma_start(out=w2s_raw[32 * q : 32 * q + 4, :].bitcast(I32), in_=w2_scales[0, 4 * q : 4 * q + 4, :].bitcast(I32))
+        for q in range(QUADRANTS):
+            nc.sync.dma_start(out=scale_rows(w2s_raw, q), in_=w2_scales[0, 4 * q : 4 * q + 4, :].bitcast(I32))
 
-        for q in range(4):
-            nc.vector.tensor_copy(out=xs_all[32 * q : 32 * q + 4, :].bitcast(I32), in_=xs_rows[32 * q : 32 * q + 4, :].bitcast(I32))
+        for q in range(QUADRANTS):
+            nc.vector.tensor_copy(out=scale_rows(xs_all, q), in_=scale_rows(xs_rows, q))
 
-        w1_bf = shared.tile([P, PACK, P, PACK], BF16, name="w1_bf", offset=4 * T, align_bytes=64)
-        views = [
-            (
-                w1_bf[:, :, ms, :].rearrange("p t m j -> p m j t"),
-                w1_raw[:].rearrange("p j (m t) -> p m j t", t=PACK)[:, ms, :, :],
-            )
-            for ms in (slice(0, 48), slice(48, P))
-        ]
-        nc.scalar.activation(out=views[0][0], in_=views[0][1], func=ACT.Copy)
+        w1_bf_offset = 4 * T
+        w1_bf = shared.tile([P, PACK, P, PACK], BF16, name="w1_bf", offset=w1_bf_offset, align_bytes=ALIGN)
+        w1_dst = w1_bf[:].rearrange("p t m j -> p m j t")
+        w1_src = w1_raw[:].rearrange("p j (m t) -> p m j t", t=PACK)
+        nc.scalar.activation(out=w1_dst[:, :SCALAR_GROUPS], in_=w1_src[:, :SCALAR_GROUPS], func=ACT.Copy)
 
-        xs = keep.tile([P, S], U8, name="xs", align_bytes=64)
+        xs = keep.tile([P, S], U8, name="xs", align_bytes=ALIGN)
         nc.vector.tensor_copy(xs[:], xs_all[:].indirect(offs_sb[:]))
-        nc.vector.tensor_copy(out=views[1][0], in_=views[1][1])
-        up_sb = keep.tile([P, PACK, S], F32, name="up_sb", tag="wide", align_bytes=64)
-        for u in range(2):
-            nc.sync.dma_start(out=up_sb[:, 2 * u : 2 * u + 2, :], in_=up_rows[:, 2 * u : 2 * u + 2, :])
-        w1c = keep.tile([P, H], U32, name="w1c", align_bytes=64)
-        w1s = keep.tile([P, H], U8, name="w1s", align_bytes=64)
+        nc.vector.tensor_copy(out=w1_dst[:, SCALAR_GROUPS:], in_=w1_src[:, SCALAR_GROUPS:])
+
+        up_sb = keep.tile([P, PACK, S], F32, name="up_sb", tag="wide", align_bytes=ALIGN)
+        for pair in range(2):
+            nc.sync.dma_start(out=up_sb[:, 2 * pair : 2 * pair + 2, :], in_=up_rows[:, 2 * pair : 2 * pair + 2, :])
+        w1c = keep.tile([P, H], U32, name="w1c", align_bytes=ALIGN)
+        w1s = keep.tile([P, H], U8, name="w1s", align_bytes=ALIGN)
         nc.vector.quantize_mx(out=w1c[:].bitcast(FP8X4), scales=w1s[:], in_=w1_bf[:].rearrange("p t m j -> p (t m j)"))
 
-        xw = [shared.tile([P, HALF], U32, name="xw%d" % h, offset=4 * T + 4 * HALF * h, align_bytes=64) for h in range(2)]
-        y_win = [keep.tile([P, S], F32, name="y_win%d" % t, align_bytes=64) for t in range(PACK)]
-        y_own = [keep.tile([P, PACK, HALF], F32, name="y_own%d" % h, align_bytes=64) for h in range(2)]
-        diff = [keep.tile([P, PACK, HALF], F32, name="diff%d" % h, align_bytes=64) for h in range(2)]
-        mag = [keep.tile([P, PACK, HALF], F32, name="mag%d" % h, align_bytes=64) for h in range(2)]
-        mid = [keep.tile([P, PACK, HALF], F32, name="mid%d" % h, align_bytes=64) for h in range(2)]
-        lift = [keep.tile([P, PACK, HALF], F32, name="lift%d" % h, align_bytes=64) for h in range(2)]
-        zb = [keep.tile([P, PIECE, PACK], BF16, name="zb%d" % c, align_bytes=64) for c in range(4)]
-        zt = [keep.tile([P, 2, P, 2], BF16, name="zt%d" % c, align_bytes=64) for c in range(2)]
-        ident = keep.tile([P, P], F32, name="ident", align_bytes=64)
+        xw = [
+            shared.tile([P, HALF], U32, name="xw%d" % h, offset=w1_bf_offset + 4 * HALF * h, align_bytes=ALIGN)
+            for h in range(2)
+        ]
+        y_win = [keep.tile([P, S], F32, name="y_win%d" % t, align_bytes=ALIGN) for t in range(PACK)]
+        y_own = [keep.tile([P, PACK, HALF], F32, name="y_own%d" % h, align_bytes=ALIGN) for h in range(2)]
+        diff = [keep.tile([P, PACK, HALF], F32, name="diff%d" % h, align_bytes=ALIGN) for h in range(2)]
+        mag = [keep.tile([P, PACK, HALF], F32, name="mag%d" % h, align_bytes=ALIGN) for h in range(2)]
+        mid = keep.tile([P, PACK, HALF], F32, name="mid", align_bytes=ALIGN)
+        lift = [keep.tile([P, PACK, HALF], F32, name="lift%d" % h, align_bytes=ALIGN) for h in range(2)]
+        zb = [keep.tile([P, PIECE, PACK], BF16, name="zb%d" % c, align_bytes=ALIGN) for c in range(S // PIECE)]
+        zt = [keep.tile([P, 2, P, 2], BF16, name="zt%d" % c, align_bytes=ALIGN) for c in range(HALF // PIECE)]
+        ident = keep.tile([P, P], F32, name="ident", align_bytes=ALIGN)
         make_identity(nc, ident[:])
-        zc = keep.tile([P, S], U32, name="zc", align_bytes=64)
-        zs = keep.tile([P, S], U8, name="zs", align_bytes=64)
-        res = keep.tile([P, PACK, S], F32, name="res", align_bytes=64)
-        rb = keep.tile([P, S, PACK], BF16, name="rb", align_bytes=64)
-        oc = keep.tile([P, S], U32, name="oc", align_bytes=64)
-        osc = keep.tile([P, S], U8, name="osc", align_bytes=64)
+        zc = keep.tile([P, S], U32, name="zc", align_bytes=ALIGN)
+        zs = keep.tile([P, S], U8, name="zs", align_bytes=ALIGN)
+        res = keep.tile([P, PACK, S], F32, name="res", align_bytes=ALIGN)
+        rb = keep.tile([P, S, PACK], BF16, name="rb", align_bytes=ALIGN)
+        oc = keep.tile([P, S], U32, name="oc", align_bytes=ALIGN)
+        osc = keep.tile([P, S], U8, name="osc", align_bytes=ALIGN)
         out_rows = out_0.rearrange("(p t) s -> p t s", t=PACK)
         out_words = out_1[0].rearrange("p c r -> p (c r)").bitcast(I32)
 
+        def bank_tag(b):
+            return "bank%d" % b
+
+        def pieces(first, count=1):
+            return slice(first * PIECE, (first + count) * PIECE)
+
+        def by_planes(ap):
+            return ap.rearrange("p t (a i) -> p a t i", i=2)
+
+        def by_words(ap):
+            return ap.rearrange("p (a i) t -> p a t i", i=2)
+
         def first_product(t, h):
-            bank = psum.tile([P, HALF], F32, name="y_bank", tag="bank%d" % (2 * t + h))
+            bank = psum.tile([P, HALF], F32, name="y_bank", tag=bank_tag(2 * t + h))
             nc.tensor.matmul_mx(
                 out=bank[:],
                 lhsT=w1c[:, t * P : (t + 1) * P].bitcast(FP8X4),
@@ -120,45 +141,44 @@ def tile_picked_cmpex_none_po_kernel(
         def own_second(t):
             nc.sync.dma_start(out=y_own[1][:, t, :], in_=y_win[t][:, HALF:S])
 
+        def list_half(lists, h):
+            return lists[:, h * HALF // LIST_ROWS : (h + 1) * HALF // LIST_ROWS]
+
         def fetch(h, t):
             nc.vector.tensor_tensor(
-                diff[h][:, t, :], y_win[t][:].indirect(mate_sb[:, h * 16 : (h + 1) * 16]), y_own[h][:, t, :], ALU.subtract
+                diff[h][:, t, :], y_win[t][:].indirect(list_half(mate_sb, h)), y_own[h][:, t, :], ALU.subtract
             )
 
-        def magnitude(h, ts, js):
-            nc.scalar.activation(out=mag[h][:, ts, js], in_=diff[h][:, ts, js], func=ACT.Abs)
+        def magnitude(h, pair):
+            ts = slice(2 * pair, 2 * pair + 2)
+            nc.scalar.activation(out=mag[h][:, ts, :], in_=diff[h][:, ts, :], func=ACT.Abs, scale=2.0 if h == 0 else 1.0)
 
-        def middle(h, ts, js):
+        def middle(js):
             nc.vector.scalar_tensor_tensor(
-                out=mid[h][:, ts, js], in0=diff[h][:, ts, js], scalar=0.5, in1=y_own[h][:, ts, js], op0=ALU.mult, op1=ALU.add
+                out=mid[:, :, js], in0=diff[1][:, :, js], scalar=0.5, in1=y_own[1][:, :, js], op0=ALU.mult, op1=ALU.add
             )
 
         def share(h, ts, js):
             nc.vector.scalar_tensor_tensor(
-                out=lift[h][:, ts, js], in0=up_sb[:, ts, h * HALF + js.start : h * HALF + js.stop], scalar=0.5, in1=mag[h][:, ts, js], op0=ALU.subtract, op1=ALU.mult
+                out=lift[h][:, ts, js],
+                in0=up_sb[:, ts, h * HALF + js.start : h * HALF + js.stop],
+                scalar=0.5,
+                in1=mag[h][:, ts, js],
+                op0=ALU.subtract,
+                op1=ALU.mult,
             )
 
         def mix(c):
-            h, js = c // 2, slice((c % 2) * PIECE, (c % 2 + 1) * PIECE)
-            nc.vector.tensor_tensor(
-                zb[c][:].rearrange("p (a i) t -> p a t i", i=2),
-                mid[h][:, :, js].rearrange("p t (a i) -> p a t i", i=2),
-                lift[h][:, :, js].rearrange("p t (a i) -> p a t i", i=2),
-                ALU.add,
-            )
+            js = pieces(c - 2)
+            nc.vector.tensor_tensor(by_words(zb[c][:]), by_planes(mid[:, :, js]), by_planes(lift[1][:, :, js]), ALU.add)
 
-        def add_turned(bank, c, t):
-            js = slice(c * PIECE, (c + 1) * PIECE)
-            nc.tensor.matmul(bank[:, t, :], mid[0][:, t, js], ident[:], start=True, stop=False, is_transpose=True)
-            nc.tensor.matmul(bank[:, t, :], lift[0][:, t, js], ident[:], start=False, stop=True, is_transpose=True)
+        def add_turned(bank, c, t, term, start=False, stop=False):
+            nc.tensor.matmul(bank[:, t, :], term[:, t, pieces(c)], ident[:], start=start, stop=stop, is_transpose=True)
 
         def turn_back(bank, c):
-            nc.scalar.copy(
-                out=zt[c][:].rearrange("j u (a i) e -> j u a e i", i=4),
-                in_=bank[:].rearrange("j (u e) (a i) -> j u a e i", e=2, i=4),
-            )
+            nc.scalar.activation(out=zt[c][:], in_=bank[:].rearrange("j (u e) p -> j u p e", e=2), func=ACT.Copy, scale=0.5)
             words = zt[c][:].rearrange("j u p e -> j u (p e)").bitcast(F32)
-            back = psum.tile([P, 2, PIECE], F32, name="back", tag="bank%d" % (2 * c))
+            back = psum.tile([P, 2, PIECE], F32, name="back", tag=bank_tag(2 * c))
             for u in range(2):
                 nc.tensor.transpose(back[:, u, :], words[:, u, :], ident[:])
             nc.scalar.copy(
@@ -167,44 +187,28 @@ def tile_picked_cmpex_none_po_kernel(
             )
 
         def quantise(codes, scales, values, cols):
-            nc.vector.quantize_mx(out=codes[:, cols].bitcast(FP8X4), scales=scales[:, cols], in_=values.rearrange("p s t -> p (s t)"))
-
-        def pass_two(dst, t, cols):
-            nc.tensor.matmul_mx(
-                out=dst,
-                lhsT=w2w[:, 2 * t * P : 2 * (t + 1) * P].bitcast(FP4X4),
-                lhsT_scale=w2s[:, t * P : (t + 1) * P],
-                rhs=zc[:, cols].bitcast(FP8X4),
-                rhs_scale=zs[:, cols],
-                start=True,
-                stop=True,
+            nc.vector.quantize_mx(
+                out=codes[:, cols].bitcast(FP8X4), scales=scales[:, cols], in_=values.rearrange("p s t -> p (s t)")
             )
 
-        def second_product(c):
-            cols = slice(c * PIECE, (c + 1) * PIECE)
+        def second_product(c, planes_a_bank):
+            cols = pieces(c)
             quantise(zc, zs, zb[c][:], cols)
-            if c < 2:
-                bank = psum.tile([P, PACK, PIECE], F32, name="o_bank", tag="bank%d" % (2 * c))
-                for t in range(PACK):
-                    pass_two(bank[:, t, :], t, cols)
-                nc.scalar.copy(out=res[:, :, cols], in_=bank[:])
-                if c == 0:
-                    nc.scalar.copy(
-                        out=rb[:, cols, :].rearrange("p (a i) t -> p a t i", i=2),
-                        in_=bank[:].rearrange("p t (a i) -> p a t i", i=2),
+            for b in range(PACK // planes_a_bank):
+                bank = psum.tile([P, planes_a_bank, PIECE], F32, name="o_bank", tag=bank_tag(2 * c + b))
+                for u in range(planes_a_bank):
+                    t = planes_a_bank * b + u
+                    nc.tensor.matmul_mx(
+                        out=bank[:, u, :],
+                        lhsT=w2w[:, 2 * t * P : 2 * (t + 1) * P].bitcast(FP4X4),
+                        lhsT_scale=w2s[:, t * P : (t + 1) * P],
+                        rhs=zc[:, cols].bitcast(FP8X4),
+                        rhs_scale=zs[:, cols],
+                        start=True,
+                        stop=True,
                     )
-            else:
-                for pair in range(2):
-                    bank = psum.tile([P, 2, PIECE], F32, name="o_bank", tag="bank%d" % (2 * c + pair))
-                    for u in range(2):
-                        pass_two(bank[:, u, :], 2 * pair + u, cols)
-                    nc.scalar.copy(out=res[:, 2 * pair : 2 * pair + 2, cols], in_=bank[:])
-
-        def round_values(cols):
-            nc.vector.tensor_copy(
-                out=rb[:, cols, :].rearrange("p (a i) t -> p a t i", i=2),
-                in_=res[:, :, cols].rearrange("p t (a i) -> p a t i", i=2),
-            )
+                nc.scalar.copy(out=res[:, planes_a_bank * b : planes_a_bank * (b + 1), cols], in_=bank[:])
+            return bank
 
         def store_values(cols):
             nc.sync.dma_start(out=out_rows[:, :, cols], in_=res[:, :, cols])
@@ -213,67 +217,71 @@ def tile_picked_cmpex_none_po_kernel(
             quantise(oc, osc, rb[:, cols, :], cols)
             nc.sync.dma_start(out=out_words[:, cols], in_=oc[:, cols].bitcast(I32))
 
-        every = slice(0, HALF)
-        all_t = slice(0, PACK)
         for h in range(2):
-            nc.vector.tensor_copy(xw[h][:], xw_all[:].bitcast(U32).indirect(offs_sb[:, h * 16 : (h + 1) * 16]))
-        w2w = shared.tile([P, 2 * N], U8, name="w2w", offset=0, align_bytes=64)
+            nc.vector.tensor_copy(xw[h][:], xw_all[:].bitcast(U32).indirect(list_half(offs_sb, h)))
+
+        w2w = shared.tile([P, 2 * N], U8, name="w2w", offset=0, align_bytes=ALIGN)
         nc.vector.tensor_copy(
             out=w2w[:].rearrange("p (t m b) -> p t m b", t=PACK, b=2),
             in_=w2w_raw[:].rearrange("p (m t b) -> p t m b", t=PACK, b=2),
         )
-
-        w2s = shared.tile([P, N], U8, name="w2s", offset=2 * N, align_bytes=64)
+        w2s = shared.tile([P, N], U8, name="w2s", offset=2 * N, align_bytes=ALIGN)
         nc.vector.tensor_copy(
             out=w2s[:].rearrange("p (t m) -> p t m", t=PACK),
             in_=w2s_raw[:].rearrange("p (m t) -> p t m", t=PACK),
         )
+
         own_first(0, first_product(0, 0))
-        ahead = first_product(1, 0)
+        plane_one = first_product(1, 0)
         for t in range(PACK):
             if t > 1:
                 own_first(t, first_product(t, 0))
             first_product(t, 1)
             if t == 0:
-                own_first(1, ahead)
+                own_first(1, plane_one)
             own_second(t)
             fetch(0, t)
-            if t > 0:
-                middle(0, slice(t - 1, t), every)
-        magnitude(0, slice(0, 2), every)
-        magnitude(0, slice(2, 4), every)
-        middle(0, slice(3, 4), every)
-        turned = [psum.tile([P, PACK, P], F32, name="turned", tag="bank%d" % (2 * c + 1)) for c in range(2)]
+        magnitude(0, 0)
+        magnitude(0, 1)
+
+        turned = [psum.tile([P, PACK, P], F32, name="turned", tag=bank_tag(2 * c + 1)) for c in range(2)]
+        for t in range(PACK):
+            for c in range(2):
+                add_turned(turned[c], c, t, y_own[0], start=(t == 0))
+                add_turned(turned[c], c, t, y_own[0])
+                add_turned(turned[c], c, t, diff[0])
         for pair in range(2):
-            share(0, slice(2 * pair, 2 * pair + 2), every)
+            share(0, slice(2 * pair, 2 * pair + 2), slice(0, HALF))
             for c in range(2):
                 for t in (2 * pair, 2 * pair + 1):
-                    add_turned(turned[c], c, t)
+                    add_turned(turned[c], c, t, lift[0], stop=(t == PACK - 1))
             fetch(1, pair)
-        magnitude(1, slice(0, 2), every)
+        magnitude(1, 0)
         fetch(1, 2)
         turn_back(turned[0], 0)
         fetch(1, 3)
-        magnitude(1, slice(2, 4), every)
+        magnitude(1, 1)
         turn_back(turned[1], 1)
-        middle(1, all_t, slice(0, 128))
-        middle(1, all_t, slice(128, 256))
-        share(1, all_t, slice(0, 128))
-        second_product(0)
-        store_values(slice(0, 128))
-        share(1, all_t, slice(128, 256))
+
+        all_planes = slice(0, PACK)
+        middle(pieces(0))
+        middle(pieces(1))
+        share(1, all_planes, pieces(0))
+        first_bank = second_product(0, PACK)
+        nc.scalar.copy(out=by_words(rb[:, pieces(0), :]), in_=by_planes(first_bank[:]))
+        store_values(pieces(0))
+        share(1, all_planes, pieces(1))
         mix(2)
-        second_product(1)
-        store_values(slice(128, 256))
+        second_product(1, PACK)
+        store_values(pieces(1))
         mix(3)
-        second_product(2)
-        store_values(slice(256, 384))
-        second_product(3)
-        store_values(slice(384, 512))
-        store_words(slice(0, 128))
-        for cols in (slice(128, 384), slice(384, 512)):
-            round_values(cols)
+        for c in (2, 3):
+            second_product(c, 2)
+            store_values(pieces(c))
+
+        store_words(pieces(0))
+        for cols in (pieces(1, 2), pieces(3)):
+            nc.vector.tensor_copy(out=by_words(rb[:, cols, :]), in_=by_planes(res[:, :, cols]))
             store_words(cols)
-        for q in range(4):
-            queue = nc.sync if q % 2 == 0 else nc.scalar
-            queue.dma_start(out=out_2[0, 4 * q : 4 * q + 4, :].bitcast(I32), in_=osc[32 * q : 32 * q + 4, :].bitcast(I32))
+        for q in range(QUADRANTS):
+            small_queue(q).dma_start(out=out_2[0, 4 * q : 4 * q + 4, :].bitcast(I32), in_=scale_rows(osc, q))

from contextlib import ExitStack

import concourse.mybir as mybir
from concourse.masks import make_identity

K, T, S, H, N = 512, 2048, 512, 512, 512
FLOPS = 2 * K * H * S + 2 * H * N * S

F32 = mybir.dt.float32
BF16 = mybir.dt.bfloat16
I32 = mybir.dt.int32
U32 = mybir.dt.uint32
U16 = mybir.dt.uint16
U8 = mybir.dt.uint8
FP8X4 = mybir.dt.float8_e4m3fn_x4
FP4X4 = mybir.dt.float4_e2m1fn_x4
ALU = mybir.AluOpType
ACT = mybir.ActivationFunctionType

P = 128
PACK = 4
QUADRANTS = 4
ALIGN = 64
LIST_ROWS = 16
HALF = S // 2
PIECE = 128
SCALAR_GROUPS = 48


def tile_picked_cmpex_none_po_kernel(
    tc, x_words, x_scales, w1, up, w2_words, w2_scales, offs, mate, out_0, out_1, out_2
):
    nc = tc.nc
    with ExitStack() as ctx:
        keep = ctx.enter_context(tc.tile_pool(name="keep", bufs=1))
        shared = ctx.enter_context(tc.tile_pool(name="shared", bufs=1))
        psum = ctx.enter_context(tc.psum_pool(name="psum", bufs=1))

        def scale_rows(tile, q):
            return tile[32 * q : 32 * q + 4, :].bitcast(I32)

        def small_queue(q):
            return nc.sync if q % 2 == 0 else nc.scalar

        offs_sb = keep.tile([P, S // LIST_ROWS], U16, name="offs_sb")
        mate_sb = keep.tile([P, S // LIST_ROWS], U16, name="mate_sb")
        xw_all = shared.tile([P, T], I32, name="xw_all", offset=0, align_bytes=ALIGN)
        xs_rows = keep.tile([P, T], U8, name="xs_rows", align_bytes=ALIGN)
        xs_all = keep.tile([P, T], U8, name="xs_all", align_bytes=ALIGN)
        w2w_raw = keep.tile([P, 2 * N], U8, name="w2w_raw", align_bytes=ALIGN)
        w2s_raw = keep.tile([P, N], U8, name="w2s_raw", align_bytes=ALIGN)
        w1_raw = keep.tile([P, PACK, H], F32, name="w1_raw", tag="wide", align_bytes=ALIGN)

        nc.vector.memset(w2s_raw[:].bitcast(I32), 0)
        nc.vector.memset(xs_all[:].bitcast(I32), 0)

        w1_rows = w1.rearrange("(p j) h -> p j h", j=PACK)
        up_rows = up.rearrange("(p t) s -> p t s", t=PACK)
        for q in range(QUADRANTS):
            small_queue(q).dma_start(out=scale_rows(xs_rows, q), in_=x_scales[0, 4 * q : 4 * q + 4, :].bitcast(I32))
        nc.sync.dma_start(offs_sb[:], offs)
        nc.sync.dma_start(out=w1_raw[:], in_=w1_rows)
        nc.sync.dma_start(out=xw_all[:], in_=x_words[0].rearrange("p c r -> p (c r)").bitcast(I32))
        nc.sync.dma_start(mate_sb[:], mate)
        nc.sync.dma_start(out=w2w_raw[:].bitcast(I32), in_=w2_words[0].bitcast(I32))
        for q in range(QUADRANTS):
            nc.sync.dma_start(out=scale_rows(w2s_raw, q), in_=w2_scales[0, 4 * q : 4 * q + 4, :].bitcast(I32))

        for q in range(QUADRANTS):
            nc.vector.tensor_copy(out=scale_rows(xs_all, q), in_=scale_rows(xs_rows, q))

        w1_bf_offset = 4 * T
        w1_bf = shared.tile([P, PACK, P, PACK], BF16, name="w1_bf", offset=w1_bf_offset, align_bytes=ALIGN)
        w1_dst = w1_bf[:].rearrange("p t m j -> p m j t")
        w1_src = w1_raw[:].rearrange("p j (m t) -> p m j t", t=PACK)
        nc.scalar.activation(out=w1_dst[:, :SCALAR_GROUPS], in_=w1_src[:, :SCALAR_GROUPS], func=ACT.Copy)

        xs = keep.tile([P, S], U8, name="xs", align_bytes=ALIGN)
        nc.vector.tensor_copy(xs[:], xs_all[:].indirect(offs_sb[:]))
        nc.vector.tensor_copy(out=w1_dst[:, SCALAR_GROUPS:], in_=w1_src[:, SCALAR_GROUPS:])

        up_sb = keep.tile([P, PACK, S], F32, name="up_sb", tag="wide", align_bytes=ALIGN)
        for pair in range(2):
            nc.sync.dma_start(out=up_sb[:, 2 * pair : 2 * pair + 2, :], in_=up_rows[:, 2 * pair : 2 * pair + 2, :])
        w1c = keep.tile([P, H], U32, name="w1c", align_bytes=ALIGN)
        w1s = keep.tile([P, H], U8, name="w1s", align_bytes=ALIGN)
        nc.vector.quantize_mx(out=w1c[:].bitcast(FP8X4), scales=w1s[:], in_=w1_bf[:].rearrange("p t m j -> p (t m j)"))

        xw = [
            shared.tile([P, HALF], U32, name="xw%d" % h, offset=w1_bf_offset + 4 * HALF * h, align_bytes=ALIGN)
            for h in range(2)
        ]
        y_win = [keep.tile([P, S], F32, name="y_win%d" % t, align_bytes=ALIGN) for t in range(PACK)]
        y_own = [keep.tile([P, PACK, HALF], F32, name="y_own%d" % h, align_bytes=ALIGN) for h in range(2)]
        diff = [keep.tile([P, PACK, HALF], F32, name="diff%d" % h, align_bytes=ALIGN) for h in range(2)]
        mag = [keep.tile([P, PACK, HALF], F32, name="mag%d" % h, align_bytes=ALIGN) for h in range(2)]
        mid = keep.tile([P, PACK, HALF], F32, name="mid", align_bytes=ALIGN)
        lift = [keep.tile([P, PACK, HALF], F32, name="lift%d" % h, align_bytes=ALIGN) for h in range(2)]
        zb = [keep.tile([P, PIECE, PACK], BF16, name="zb%d" % c, align_bytes=ALIGN) for c in range(S // PIECE)]
        zt = [keep.tile([P, 2, P, 2], BF16, name="zt%d" % c, align_bytes=ALIGN) for c in range(HALF // PIECE)]
        ident = keep.tile([P, P], F32, name="ident", align_bytes=ALIGN)
        make_identity(nc, ident[:])
        zc = keep.tile([P, S], U32, name="zc", align_bytes=ALIGN)
        zs = keep.tile([P, S], U8, name="zs", align_bytes=ALIGN)
        res = keep.tile([P, PACK, S], F32, name="res", align_bytes=ALIGN)
        rb = keep.tile([P, S, PACK], BF16, name="rb", align_bytes=ALIGN)
        oc = keep.tile([P, S], U32, name="oc", align_bytes=ALIGN)
        osc = keep.tile([P, S], U8, name="osc", align_bytes=ALIGN)
        out_rows = out_0.rearrange("(p t) s -> p t s", t=PACK)
        out_words = out_1[0].rearrange("p c r -> p (c r)").bitcast(I32)

        def bank_tag(b):
            return "bank%d" % b

        def pieces(first, count=1):
            return slice(first * PIECE, (first + count) * PIECE)

        def by_planes(ap):
            return ap.rearrange("p t (a i) -> p a t i", i=2)

        def by_words(ap):
            return ap.rearrange("p (a i) t -> p a t i", i=2)

        def first_product(t, h):
            bank = psum.tile([P, HALF], F32, name="y_bank", tag=bank_tag(2 * t + h))
            nc.tensor.matmul_mx(
                out=bank[:],
                lhsT=w1c[:, t * P : (t + 1) * P].bitcast(FP8X4),
                lhsT_scale=w1s[:, t * P : (t + 1) * P],
                rhs=xw[h][:].bitcast(FP8X4),
                rhs_scale=xs[:, h * HALF : (h + 1) * HALF],
                start=True,
                stop=True,
            )
            nc.scalar.copy(out=y_win[t][:, h * HALF : (h + 1) * HALF], in_=bank[:])
            return bank

        def own_first(t, bank):
            nc.scalar.copy(out=y_own[0][:, t, :], in_=bank[:])

        def own_second(t):
            nc.sync.dma_start(out=y_own[1][:, t, :], in_=y_win[t][:, HALF:S])

        def list_half(lists, h):
            return lists[:, h * HALF // LIST_ROWS : (h + 1) * HALF // LIST_ROWS]

        def fetch(h, t):
            nc.vector.tensor_tensor(
                diff[h][:, t, :], y_win[t][:].indirect(list_half(mate_sb, h)), y_own[h][:, t, :], ALU.subtract
            )

        def magnitude(h, pair):
            ts = slice(2 * pair, 2 * pair + 2)
            nc.scalar.activation(out=mag[h][:, ts, :], in_=diff[h][:, ts, :], func=ACT.Abs, scale=2.0 if h == 0 else 1.0)

        def middle(js):
            nc.vector.scalar_tensor_tensor(
                out=mid[:, :, js], in0=diff[1][:, :, js], scalar=0.5, in1=y_own[1][:, :, js], op0=ALU.mult, op1=ALU.add
            )

        def share(h, ts, js):
            nc.vector.scalar_tensor_tensor(
                out=lift[h][:, ts, js],
                in0=up_sb[:, ts, h * HALF + js.start : h * HALF + js.stop],
                scalar=0.5,
                in1=mag[h][:, ts, js],
                op0=ALU.subtract,
                op1=ALU.mult,
            )

        def mix(c):
            js = pieces(c - 2)
            nc.vector.tensor_tensor(by_words(zb[c][:]), by_planes(mid[:, :, js]), by_planes(lift[1][:, :, js]), ALU.add)

        def add_turned(bank, c, t, term, start=False, stop=False):
            nc.tensor.matmul(bank[:, t, :], term[:, t, pieces(c)], ident[:], start=start, stop=stop, is_transpose=True)

        def turn_back(bank, c):
            nc.scalar.activation(out=zt[c][:], in_=bank[:].rearrange("j (u e) p -> j u p e", e=2), func=ACT.Copy, scale=0.5)
            words = zt[c][:].rearrange("j u p e -> j u (p e)").bitcast(F32)
            back = psum.tile([P, 2, PIECE], F32, name="back", tag=bank_tag(2 * c))
            for u in range(2):
                nc.tensor.transpose(back[:, u, :], words[:, u, :], ident[:])
            nc.scalar.copy(
                out=zb[c][:].rearrange("p s t -> p (s t)").bitcast(F32).rearrange("p (a i u) -> p a u i", i=2, u=2),
                in_=back[:].rearrange("p u (a i) -> p a u i", i=2),
            )

        def quantise(codes, scales, values, cols):
            nc.vector.quantize_mx(
                out=codes[:, cols].bitcast(FP8X4), scales=scales[:, cols], in_=values.rearrange("p s t -> p (s t)")
            )

        def second_product(c, planes_a_bank):
            cols = pieces(c)
            quantise(zc, zs, zb[c][:], cols)
            for b in range(PACK // planes_a_bank):
                bank = psum.tile([P, planes_a_bank, PIECE], F32, name="o_bank", tag=bank_tag(2 * c + b))
                for u in range(planes_a_bank):
                    t = planes_a_bank * b + u
                    nc.tensor.matmul_mx(
                        out=bank[:, u, :],
                        lhsT=w2w[:, 2 * t * P : 2 * (t + 1) * P].bitcast(FP4X4),
                        lhsT_scale=w2s[:, t * P : (t + 1) * P],
                        rhs=zc[:, cols].bitcast(FP8X4),
                        rhs_scale=zs[:, cols],
                        start=True,
                        stop=True,
                    )
                nc.scalar.copy(out=res[:, planes_a_bank * b : planes_a_bank * (b + 1), cols], in_=bank[:])
            return bank

        def store_values(cols):
            nc.sync.dma_start(out=out_rows[:, :, cols], in_=res[:, :, cols])

        def store_words(cols):
            quantise(oc, osc, rb[:, cols, :], cols)
            nc.sync.dma_start(out=out_words[:, cols], in_=oc[:, cols].bitcast(I32))

        for h in range(2):
            nc.vector.tensor_copy(xw[h][:], xw_all[:].bitcast(U32).indirect(list_half(offs_sb, h)))

        w2w = shared.tile([P, 2 * N], U8, name="w2w", offset=0, align_bytes=ALIGN)
        nc.vector.tensor_copy(
            out=w2w[:].rearrange("p (t m b) -> p t m b", t=PACK, b=2),
            in_=w2w_raw[:].rearrange("p (m t b) -> p t m b", t=PACK, b=2),
        )
        w2s = shared.tile([P, N], U8, name="w2s", offset=2 * N, align_bytes=ALIGN)
        nc.vector.tensor_copy(
            out=w2s[:].rearrange("p (t m) -> p t m", t=PACK),
            in_=w2s_raw[:].rearrange("p (m t) -> p t m", t=PACK),
        )

        own_first(0, first_product(0, 0))
        plane_one = first_product(1, 0)
        for t in range(PACK):
            if t > 1:
                own_first(t, first_product(t, 0))
            first_product(t, 1)
            if t == 0:
                own_first(1, plane_one)
            own_second(t)
            fetch(0, t)
        magnitude(0, 0)
        magnitude(0, 1)

        turned = [psum.tile([P, PACK, P], F32, name="turned", tag=bank_tag(2 * c + 1)) for c in range(2)]
        for t in range(PACK):
            for c in range(2):
                add_turned(turned[c], c, t, y_own[0], start=(t == 0))
                add_turned(turned[c], c, t, y_own[0])
                add_turned(turned[c], c, t, diff[0])
        for pair in range(2):
            share(0, slice(2 * pair, 2 * pair + 2), slice(0, HALF))
            for c in range(2):
                for t in (2 * pair, 2 * pair + 1):
                    add_turned(turned[c], c, t, lift[0], stop=(t == PACK - 1))
            fetch(1, pair)
        magnitude(1, 0)
        fetch(1, 2)
        turn_back(turned[0], 0)
        fetch(1, 3)
        magnitude(1, 1)
        turn_back(turned[1], 1)

        all_planes = slice(0, PACK)
        middle(pieces(0))
        middle(pieces(1))
        share(1, all_planes, pieces(0))
        first_bank = second_product(0, PACK)
        nc.scalar.copy(out=by_words(rb[:, pieces(0), :]), in_=by_planes(first_bank[:]))
        store_values(pieces(0))
        share(1, all_planes, pieces(1))
        mix(2)
        second_product(1, PACK)
        store_values(pieces(1))
        mix(3)
        for c in (2, 3):
            second_product(c, 2)
            store_values(pieces(c))

        store_words(pieces(0))
        for cols in (pieces(1, 2), pieces(3)):
            nc.vector.tensor_copy(out=by_words(rb[:, cols, :]), in_=by_planes(res[:, :, cols]))
            store_words(cols)
        for q in range(QUADRANTS):
            small_queue(q).dma_start(out=out_2[0, 4 * q : 4 * q + 4, :].bitcast(I32), in_=scale_rows(osc, q))
